import numpy as np, ml_dtypes
CORES = [7,15,23,31,39,47,55,63,71,79]
N = 10
COUNTS = [[0,0,204,816,102,0,102,0,102,0],[0,0,102,816,102,0,102,102,102,0],[0,0,0,816,204,0,102,102,0,204],[102,102,0,0,204,102,0,0,102,0],[0,102,102,816,0,204,102,0,0,204],[0,204,0,816,0,0,102,204,204,204],[204,102,0,816,102,102,0,0,204,0],[0,102,204,816,0,204,204,0,204,102],[102,204,204,816,0,0,102,204,0,0],[204,0,204,816,204,0,204,0,102,0]]
XW, YW = 1836, 7344
def setup_inputs(rng):
    return {"x": rng.standard_normal((N, 128, XW), dtype=np.float32).astype(ml_dtypes.bfloat16)}
def reference(x):
    y = np.full((N, 128, YW), np.nan, x.dtype)
    fill = [0] * N
    for s in range(N):
        o = 0
        for d in range(N):
            c = COUNTS[s][d]
            y[d][:, fill[d]:fill[d] + c] = x[s][:, o:o + c]
            o += c; fill[d] += c
    return {"y": y}

@@ -1,0 +1,32 @@
+SCRATCH = {
+    "xs": ("sbuf", [128, 1836], "bfloat16"),
+    "land": ("sbuf", [128, 7344], "bfloat16"),
+}
+SEMAPHORES = ["loaded", "sent", "arrived", "stored"]
+
+
+def rank_program(g, core, T, topo):
+    rank = T.rank_of(core)
+    if rank is None:
+        return
+    C = T.tables["COUNTS"]
+    n = len(C)
+    used = sum(C[rank])
+    g.dma_start(T.xs[:, 0:used], T.x[:, 0:used]).then_inc(T.sem.loaded, 16)
+    g.wait_ge(T.sem.loaded, 16)
+    o = 0
+    sent = 0
+    for d in range(n):
+        c = C[rank][d]
+        if c:
+            fill = sum(C[s][d] for s in range(rank))
+            rid, pid, _se = topo.addr(T.cores[d])
+            g.remote_dma(T.land[:, fill:fill + c], T.xs[:, o:o + c], T.sem.arrived, T.sem.sent, pid, rid, 0xFF)
+            sent += 8
+        o += c
+    g.wait_ge(T.sem.sent, sent)
+    inc = 8 * sum(1 for s in range(n) if C[s][rank])
+    tot = sum(C[s][rank] for s in range(n))
+    g.wait_ge(T.sem.arrived, inc)
+    g.dma_start(T.y[:, 0:tot], T.land[:, 0:tot]).then_inc(T.sem.stored, 16)
+    g.wait_ge(T.sem.stored, 16)

@@ -1,32 +1,176 @@
 SCRATCH = {
     "xs": ("sbuf", [128, 1836], "bfloat16"),
     "land": ("sbuf", [128, 7344], "bfloat16"),
+    "buf": ("sbuf", [128, 1536], "bfloat16"),
 }
-SEMAPHORES = ["loaded", "sent", "arrived", "stored"]
+SEMAPHORES = ["ld0", "ld1", "ld2", "ld3", "in0", "in1", "in2", "arr0", "arr1", "arr2", "sent", "st"]
+
+NSTAGE = 3
+OFF_CHIP = 0x00FF
+ON_CHIP = 0xFF00
+ENGINES = 8
+
+
+def share(total, n):
+    return [total // n + (1 if i < total % n else 0) for i in range(n)]
+
+
+def build_plan(C, cores):
+    n = len(C)
+    chip = [c // 8 for c in cores]
+    helper = [8 * ch + 3 for ch in chip]
+    tot = [sum(C[s][d] for s in range(n)) for d in range(n)]
+    hot = max(range(n), key=lambda d: tot[d])
+    pal = [r for r in range(n) if chip[r] == chip[hot] ^ 1][0]
+    relay0, relay1 = 8 * chip[pal] + 6, 8 * chip[pal] + 2
+    near = [s for s in range(n) if s not in (hot, pal) and (chip[s] ^ chip[hot]) & 1 == 0]
+    far = [s for s in range(n) if s not in (hot, pal) and (chip[s] ^ chip[hot]) & 1 == 1]
+
+    port = -(-sum(C[s][hot] + C[s][pal] for s in near + far) // 4)
+    a_tot = sum(C[s][hot] for s in near) - port
+    p_tot = port - sum(C[s][pal] for s in near)
+    q_tot = port - sum(C[s][pal] for s in far)
+    a_w = dict(zip(near, share(a_tot, len(near))))
+    p_w = dict(zip(far, share(p_tot, len(far))))
+    q_w = dict(zip(far, share(q_tot, len(far))))
+    own1 = min(C[pal][hot], port - q_tot)
+    cross = [d for d in near if C[pal][d]]
+    detour = min(cross, key=lambda d: C[pal][d]) if cross else None
+
+    pieces = []
+    for s in range(n):
+        xo = 0
+        for d in range(n):
+            w = C[s][d]
+            yo = sum(C[t][d] for t in range(s))
+            src, dst = cores[s], cores[d]
+            if w and d == hot:
+                if s in near:
+                    parts = [(w - a_w[s], [helper[s]], True), (a_w[s], [], True)]
+                elif s in far:
+                    parts = [(q_w[s], [helper[s], relay1], True), (p_w[s], [relay0], True),
+                             (w - q_w[s] - p_w[s], [], False)]
+                else:
+                    parts = [(own1, [helper[s]], True), (w - own1, [], True)]
+                stages = [[], []]
+                for pw, via, cut in parts:
+                    if cut:
+                        stages[0].append((pw - pw // 2, via))
+                        stages[1].append((pw // 2, via))
+                    else:
+                        stages[0].append((pw, via))
+                order = [0, 1]
+                if sum(1 for t in range(s) if C[t][d]) % 2:
+                    order = [1, 0]
+                o = 0
+                for st in order:
+                    for pw, via in stages[st]:
+                        if pw:
+                            pieces.append({"s": s, "d": d, "xo": xo + o, "yo": yo + o, "w": pw, "stage": st,
+                                           "path": [src] + via + [dst]})
+                            o += pw
+            elif w:
+                via = []
+                if d == pal and s in far:
+                    via = [helper[s]]
+                elif s == pal and d == detour:
+                    via = [8 * (chip[d] ^ 1) + 6]
+                pieces.append({"s": s, "d": d, "xo": xo, "yo": yo, "w": w, "stage": 2, "path": [src] + via + [dst]})
+            xo += w
+    return pieces
+
+
+def build_writes(pieces):
+    top = {}
+    writes = []
+    for p in pieces:
+        path = p["path"]
+        so = p["xo"]
+        for h in range(len(path) - 1):
+            last = h == len(path) - 2
+            if last:
+                do = p["yo"]
+            else:
+                do = top.get(path[h + 1], 0)
+                top[path[h + 1]] = do + p["w"]
+            writes.append({"src": path[h], "dst": path[h + 1], "stage": p["stage"], "hop": h, "w": p["w"],
+                           "so": so, "do": do, "first": h == 0, "last": last, "left": len(path) - 1 - h})
+            so = do
+    return writes
+
+
+def merged(ranges):
+    out = []
+    for lo, hi in sorted(ranges):
+        if out and out[-1][1] == lo:
+            out[-1] = (out[-1][0], hi)
+        else:
+            out.append((lo, hi))
+    return out
 
 
 def rank_program(g, core, T, topo):
-    rank = T.rank_of(core)
-    if rank is None:
-        return
     C = T.tables["COUNTS"]
-    n = len(C)
-    used = sum(C[rank])
-    g.dma_start(T.xs[:, 0:used], T.x[:, 0:used]).then_inc(T.sem.loaded, 16)
-    g.wait_ge(T.sem.loaded, 16)
-    o = 0
+    cores = list(T.cores)
+    pieces = build_plan(C, cores)
+    writes = build_writes(pieces)
+    mine = [w for w in writes if w["src"] == core]
+    coming = [w for w in writes if w["dst"] == core]
+    if not mine and not coming:
+        return
+    rank = T.rank_of(core)
+    queues = [g.sync, g.scalar]
+
+    loads = {}
+    if rank is not None:
+        k = 0
+        for st in range(NSTAGE):
+            for lo, hi in merged([(p["xo"], p["xo"] + p["w"]) for p in pieces if p["s"] == rank and p["stage"] == st]):
+                sem = T.sem["ld%d" % k]
+                queues[k % 2].dma_start(T.xs[:, lo:hi], T.x[:, lo:hi]).then_inc(sem, 16)
+                loads.setdefault(st, []).append(sem)
+                k += 1
+
     sent = 0
-    for d in range(n):
-        c = C[rank][d]
-        if c:
-            fill = sum(C[s][d] for s in range(rank))
-            rid, pid, _se = topo.addr(T.cores[d])
-            g.remote_dma(T.land[:, fill:fill + c], T.xs[:, o:o + c], T.sem.arrived, T.sem.sent, pid, rid, 0xFF)
-            sent += 8
-        o += c
-    g.wait_ge(T.sem.sent, sent)
-    inc = 8 * sum(1 for s in range(n) if C[s][rank])
-    tot = sum(C[s][rank] for s in range(n))
-    g.wait_ge(T.sem.arrived, inc)
-    g.dma_start(T.y[:, 0:tot], T.land[:, 0:tot]).then_inc(T.sem.stored, 16)
-    g.wait_ge(T.sem.stored, 16)
+    for st in range(NSTAGE):
+        batch = sorted([w for w in mine if w["stage"] == st], key=lambda w: -w["left"])
+        if not batch:
+            continue
+        for sem in loads.get(st, []):
+            g.wait_ge(sem, 16)
+        passing = sum(ENGINES for w in coming if w["stage"] == st and not w["last"])
+        if passing:
+            g.wait_ge(T.sem["in%d" % st], passing)
+        for w in batch:
+            src = T.xs if w["first"] else T.buf
+            dst = T.land if w["last"] else T.buf
+            sem = T.sem["arr%d" % st] if w["last"] else T.sem["in%d" % st]
+            rid, pid, se = topo.addr(w["dst"])
+            mask = ON_CHIP if topo.chip(core) == topo.chip(w["dst"]) else OFF_CHIP
+            g.remote_dma(dst[:, w["do"]:w["do"] + w["w"]], src[:, w["so"]:w["so"] + w["w"]], sem, T.sem.sent,
+                         pid, rid, mask)
+            sent += ENGINES
+    if sent:
+        g.wait_ge(T.sem.sent, sent)
+
+    if rank is not None:
+        stored = 0
+        k = 0
+        for st in range(NSTAGE):
+            here = [w for w in coming if w["stage"] == st and w["last"]]
+            if not here:
+                continue
+            sem, need = T.sem["arr%d" % st], ENGINES * len(here)
+            ranges = merged([(w["do"], w["do"] + w["w"]) for w in here])
+            waited = set()
+            for lo, hi in ranges:
+                q = k % 2
+                if q not in waited:
+                    queues[q].wait_ge(sem, need)
+                    waited.add(q)
+                queues[q].dma_start(T.y[:, lo:hi], T.land[:, lo:hi]).then_inc(T.sem.st, 16)
+                stored += 16
+                k += 1
+            g.wait_ge(sem, need)
+        if stored:
+            g.wait_ge(T.sem.st, stored)

SCRATCH = {
    "xs": ("sbuf", [128, 1836], "bfloat16"),
    "land": ("sbuf", [128, 7344], "bfloat16"),
    "buf": ("sbuf", [128, 1536], "bfloat16"),
}
SEMAPHORES = ["ld0", "ld1", "ld2", "ld3", "in0", "in1", "in2", "arr0", "arr1", "arr2", "sent", "st"]

NSTAGE = 3
OFF_CHIP = 0x00FF
ON_CHIP = 0xFF00
ENGINES = 8


def share(total, n):
    return [total // n + (1 if i < total % n else 0) for i in range(n)]


def build_plan(C, cores):
    n = len(C)
    chip = [c // 8 for c in cores]
    helper = [8 * ch + 3 for ch in chip]
    tot = [sum(C[s][d] for s in range(n)) for d in range(n)]
    hot = max(range(n), key=lambda d: tot[d])
    pal = [r for r in range(n) if chip[r] == chip[hot] ^ 1][0]
    relay0, relay1 = 8 * chip[pal] + 6, 8 * chip[pal] + 2
    near = [s for s in range(n) if s not in (hot, pal) and (chip[s] ^ chip[hot]) & 1 == 0]
    far = [s for s in range(n) if s not in (hot, pal) and (chip[s] ^ chip[hot]) & 1 == 1]

    port = -(-sum(C[s][hot] + C[s][pal] for s in near + far) // 4)
    a_tot = sum(C[s][hot] for s in near) - port
    p_tot = port - sum(C[s][pal] for s in near)
    q_tot = port - sum(C[s][pal] for s in far)
    a_w = dict(zip(near, share(a_tot, len(near))))
    p_w = dict(zip(far, share(p_tot, len(far))))
    q_w = dict(zip(far, share(q_tot, len(far))))
    own1 = min(C[pal][hot], port - q_tot)
    cross = [d for d in near if C[pal][d]]
    detour = min(cross, key=lambda d: C[pal][d]) if cross else None

    pieces = []
    for s in range(n):
        xo = 0
        for d in range(n):
            w = C[s][d]
            yo = sum(C[t][d] for t in range(s))
            src, dst = cores[s], cores[d]
            if w and d == hot:
                if s in near:
                    parts = [(w - a_w[s], [helper[s]], True), (a_w[s], [], True)]
                elif s in far:
                    parts = [(q_w[s], [helper[s], relay1], True), (p_w[s], [relay0], True),
                             (w - q_w[s] - p_w[s], [], False)]
                else:
                    parts = [(own1, [helper[s]], True), (w - own1, [], True)]
                stages = [[], []]
                for pw, via, cut in parts:
                    if cut:
                        stages[0].append((pw - pw // 2, via))
                        stages[1].append((pw // 2, via))
                    else:
                        stages[0].append((pw, via))
                order = [0, 1]
                if sum(1 for t in range(s) if C[t][d]) % 2:
                    order = [1, 0]
                o = 0
                for st in order:
                    for pw, via in stages[st]:
                        if pw:
                            pieces.append({"s": s, "d": d, "xo": xo + o, "yo": yo + o, "w": pw, "stage": st,
                                           "path": [src] + via + [dst]})
                            o += pw
            elif w:
                via = []
                if d == pal and s in far:
                    via = [helper[s]]
                elif s == pal and d == detour:
                    via = [8 * (chip[d] ^ 1) + 6]
                pieces.append({"s": s, "d": d, "xo": xo, "yo": yo, "w": w, "stage": 2, "path": [src] + via + [dst]})
            xo += w
    return pieces


def build_writes(pieces):
    top = {}
    writes = []
    for p in pieces:
        path = p["path"]
        so = p["xo"]
        for h in range(len(path) - 1):
            last = h == len(path) - 2
            if last:
                do = p["yo"]
            else:
                do = top.get(path[h + 1], 0)
                top[path[h + 1]] = do + p["w"]
            writes.append({"src": path[h], "dst": path[h + 1], "stage": p["stage"], "hop": h, "w": p["w"],
                           "so": so, "do": do, "first": h == 0, "last": last, "left": len(path) - 1 - h})
            so = do
    return writes


def merged(ranges):
    out = []
    for lo, hi in sorted(ranges):
        if out and out[-1][1] == lo:
            out[-1] = (out[-1][0], hi)
        else:
            out.append((lo, hi))
    return out


def rank_program(g, core, T, topo):
    C = T.tables["COUNTS"]
    cores = list(T.cores)
    pieces = build_plan(C, cores)
    writes = build_writes(pieces)
    mine = [w for w in writes if w["src"] == core]
    coming = [w for w in writes if w["dst"] == core]
    if not mine and not coming:
        return
    rank = T.rank_of(core)
    queues = [g.sync, g.scalar]

    loads = {}
    if rank is not None:
        k = 0
        for st in range(NSTAGE):
            for lo, hi in merged([(p["xo"], p["xo"] + p["w"]) for p in pieces if p["s"] == rank and p["stage"] == st]):
                sem = T.sem["ld%d" % k]
                queues[k % 2].dma_start(T.xs[:, lo:hi], T.x[:, lo:hi]).then_inc(sem, 16)
                loads.setdefault(st, []).append(sem)
                k += 1

    sent = 0
    for st in range(NSTAGE):
        batch = sorted([w for w in mine if w["stage"] == st], key=lambda w: -w["left"])
        if not batch:
            continue
        for sem in loads.get(st, []):
            g.wait_ge(sem, 16)
        passing = sum(ENGINES for w in coming if w["stage"] == st and not w["last"])
        if passing:
            g.wait_ge(T.sem["in%d" % st], passing)
        for w in batch:
            src = T.xs if w["first"] else T.buf
            dst = T.land if w["last"] else T.buf
            sem = T.sem["arr%d" % st] if w["last"] else T.sem["in%d" % st]
            rid, pid, se = topo.addr(w["dst"])
            mask = ON_CHIP if topo.chip(core) == topo.chip(w["dst"]) else OFF_CHIP
            g.remote_dma(dst[:, w["do"]:w["do"] + w["w"]], src[:, w["so"]:w["so"] + w["w"]], sem, T.sem.sent,
                         pid, rid, mask)
            sent += ENGINES
    if sent:
        g.wait_ge(T.sem.sent, sent)

    if rank is not None:
        stored = 0
        k = 0
        for st in range(NSTAGE):
            here = [w for w in coming if w["stage"] == st and w["last"]]
            if not here:
                continue
            sem, need = T.sem["arr%d" % st], ENGINES * len(here)
            ranges = merged([(w["do"], w["do"] + w["w"]) for w in here])
            waited = set()
            for lo, hi in ranges:
                q = k % 2
                if q not in waited:
                    queues[q].wait_ge(sem, need)
                    waited.add(q)
                queues[q].dma_start(T.y[:, lo:hi], T.land[:, lo:hi]).then_inc(T.sem.st, 16)
                stored += 16
                k += 1
            g.wait_ge(sem, need)
        if stored:
            g.wait_ge(T.sem.st, stored)
